import numpy as np
import ml_dtypes


def mxq(x, axis, fmt="e4m3"):
    dtype, down = {"e4m3": (ml_dtypes.float8_e4m3fn, 7), "e5m2": (ml_dtypes.float8_e5m2, 14)}[fmt]
    v = np.moveaxis(np.asarray(x, np.float32).astype(ml_dtypes.bfloat16).astype(np.float64), axis, -1)
    blocks = v.reshape(v.shape[:-1] + (-1, 32))
    amax = np.abs(blocks).max(-1, keepdims=True)
    byte = np.maximum(np.where(amax > 0, np.frexp(amax)[1] - 1 + 127, 0) - down, 1)
    scale = np.exp2(byte - 127.0)
    codes = (blocks / scale).astype(np.float32).astype(dtype).astype(np.float64)
    return np.moveaxis((codes * scale).reshape(v.shape), -1, axis)


WIDE = False


def mx_kscale(k):
    if not WIDE:
        return np.ones(k)
    levels = np.array([10, -10, 5, -5, 0])
    if k % 512:
        return np.exp2(np.random.permutation(np.resize(levels, k // 32))).repeat(32)
    a = np.empty((k // 512, 16))
    for p in range(k // 512):
        a[p, :8] = np.random.permutation(np.resize(levels, 8))
        for g in range(8):
            far = levels[np.abs(levels - a[p, g]) >= 10]
            a[p, g + 8] = far[np.random.randint(len(far))]
    return np.exp2(a.ravel()).repeat(32)


def f64(x):
    return np.asarray(x).astype(np.float64)


def striped(idx):
    return np.tile(idx.reshape(-1, 16).T, (8, 1)).astype(np.uint16)


def unstriped(offs):
    return offs[:16].T.reshape(-1).astype(np.int64)


E2M1 = np.array([0.0, 0.5, 1.0, 1.5, 2.0, 3.0, 4.0, 6.0, -0.0, -0.5, -1.0, -1.5, -2.0, -3.0, -4.0, -6.0])


def pack_weight(w, fmt):
    k, n = w.shape
    w = f64(np.asarray(w, np.float32).astype(ml_dtypes.bfloat16)).reshape(k // 32, 32, n)
    amax = np.abs(w).max(1)
    if fmt == "e4m3":
        byte = np.frexp(amax)[1] - 1 + 127 - 7
    else:
        mant, ex = np.frexp(amax / 6.0)
        byte = np.where(mant > 0.5, ex, ex - 1) + 127
    byte = np.clip(np.where(amax > 0, byte, 1), 1, 254)
    scaled = (w * np.exp2(127.0 - byte)[:, None, :]).reshape(k, n).astype(np.float32)
    by_word = np.ascontiguousarray(scaled.reshape(k // 512, 128, 4, n).transpose(0, 1, 3, 2))
    if fmt == "e4m3":
        words = by_word.astype(ml_dtypes.float8_e4m3fn).view(np.uint8)
    else:
        c = by_word.astype(ml_dtypes.float4_e2m1fn).view(np.uint8) & 0xF
        words = (c[..., 0::2] | (c[..., 1::2] << 4)).reshape(k // 512, 128, 2 * n)
    return np.ascontiguousarray(words), np.ascontiguousarray(byte.astype(np.uint8).reshape(k // 512, 16, n))


def unpack_weight(words, scales, fmt):
    g, _, n = scales.shape
    words = np.ascontiguousarray(words).reshape(g, 128, n, -1)
    if fmt == "e4m3":
        vals = words.view(ml_dtypes.float8_e4m3fn).astype(np.float64)
    else:
        nib = np.empty((g, 128, n, 4), np.uint8)
        nib[..., 0::2] = words & 0xF
        nib[..., 1::2] = words >> 4
        vals = E2M1[nib]
    vals = vals * np.repeat(np.exp2(scales.astype(np.float64) - 127.0), 8, axis=1)[..., None]
    return vals.transpose(0, 1, 3, 2).reshape(g * 512, n)


K, T, E, C, N = 512, 1024, 6, 256, 128


def by_expert(wq, xq):
    return np.concatenate([wq[e].T @ xq[:, e * C:(e + 1) * C] for e in range(E)], axis=1)


def setup_inputs():
    n = np.random.standard_normal
    s = mx_kscale(K)[:, None]
    w = [pack_weight(m, "e2m1") for m in n((E, K, N)) / np.sqrt(K) / s[None]]
    idx = np.random.permutation(E * C)
    return {
        "xT": (n((K, T)) * s).astype(np.float32),
        "w_words": np.stack([m[0] for m in w]),
        "w_scales": np.stack([m[1] for m in w]),
        "b": (0.3 * n((N, E))).astype(np.float32),
        "gate": np.tile(np.where(idx < T, np.random.uniform(0.2, 1.0, E * C), 0.0), (N, 1)).astype(np.float32),
        "offs": striped(idx),
    }


def reference(xT, w_words, w_scales, b, gate, offs):
    idx = unstriped(offs)
    w = np.stack([unpack_weight(w_words[e], w_scales[e], "e2m1") for e in range(E)])
    xq = mxq(np.concatenate([f64(xT), np.zeros((K, E * C - T))], axis=1)[:, idx], 0, "e4m3")
    y = by_expert(w, xq)
    y = y + np.repeat(f64(b), C, axis=1)
    out = np.zeros((N, E * C))
    out[:, idx] = f64(gate) * y
    return out[:, :T]

@@ -1,0 +1,144 @@
+from contextlib import ExitStack
+
+import concourse.mybir as mybir
+
+K, T, E, C, N = 512, 1024, 6, 256, 128
+S = E * C
+P = 128
+FLOPS = 2 * K * N * S
+
+F32 = mybir.dt.float32
+BF16 = mybir.dt.bfloat16
+I32 = mybir.dt.int32
+U32 = mybir.dt.uint32
+U16 = mybir.dt.uint16
+U8 = mybir.dt.uint8
+FP8X4 = mybir.dt.float8_e4m3fn_x4
+FP4X4 = mybir.dt.float4_e2m1fn_x4
+COPY = mybir.ActivationFunctionType.Copy
+IDENT = mybir.ActivationFunctionType.Identity
+MULT = mybir.AluOpType.mult
+
+PAIR_CHUNKS = [(0, 640), (640, 1024)]
+LAST_ROW_CHUNKS = [(0, 512), (512, 1024)]
+GATE_CHUNKS = [(0, 1), (1, 3), (3, 6)]
+EARLY = 3
+LOW_AT = [0, 2, 3, 4, 0, 1]
+HIGH_AT = [1, 5, 6, 5, 6, 5]
+
+
+def tile_moe_pad_lin_bias_kernel(tc, xT, w_words, w_scales, b, gate, offs, out):
+    nc = tc.nc
+    with ExitStack() as ctx:
+        keep = ctx.enter_context(tc.tile_pool(name="keep", bufs=1))
+        psum = ctx.enter_context(tc.psum_pool(name="psum", bufs=1))
+
+        x_rows = xT.rearrange("(p j) t -> p j t", j=4)
+        offsets = keep.tile([P, S // 16], U16, name="offsets")
+        pairs = keep.tile([P, 2 * S], BF16, name="pairs", align_bytes=64)
+        row2 = keep.tile([P, S], BF16, name="row2", align_bytes=64)
+        row3 = keep.tile([P, S], BF16, name="row3", align_bytes=64)
+        raw_pairs = [keep.tile([P, 2, hi - lo], F32, name=f"raw_pair{lo}") for lo, hi in PAIR_CHUNKS]
+        raw2 = keep.tile([P, T], F32, name="raw2")
+        raw3 = [keep.tile([P, hi - lo], F32, name=f"raw3_{lo}") for lo, hi in LAST_ROW_CHUNKS]
+        w_sb = keep.tile([P, E, 2 * N], U8, name="w_sb", align_bytes=64)
+        ws_sb = keep.tile([P, E, N], U8, name="ws_sb", align_bytes=64)
+        b_sb = keep.tile([P, E], F32, name="b_sb")
+        gate_sb = [keep.tile([P, (hi - lo) * C], F32, name=f"gate{lo}") for lo, hi in GATE_CHUNKS]
+        result = keep.tile([P, S], F32, name="result")
+
+        nc.vector.memset(pairs[:, 2 * T:].bitcast(I32), 0)
+        nc.vector.memset(ws_sb[:].rearrange("p e n -> p (e n)").bitcast(I32), 0)
+        nc.gpsimd.memset(row3[:, T:], 0.0)
+        nc.scalar.dma_start(b_sb[:], b)
+        nc.scalar.activation(row2[:, T:], pairs[:, 2 * T:2 * T + S - T], COPY)
+
+        nc.sync.dma_start(raw2[:], x_rows[:, 2, :])
+        nc.sync.dma_start(offsets[:], offs)
+        for raw, (lo, hi) in zip(raw_pairs, PAIR_CHUNKS):
+            nc.sync.dma_start(raw[:], x_rows[:, 0:2, lo:hi])
+        ws_rows = w_scales.rearrange("e a q n -> q (e a) n").bitcast(I32)
+        for quad in range(4):
+            nc.sync.dma_start(ws_sb[32 * quad:32 * quad + 4].bitcast(I32), ws_rows[4 * quad:4 * quad + 4])
+        for raw, (lo, hi) in zip(raw3, LAST_ROW_CHUNKS):
+            nc.sync.dma_start(raw[:], x_rows[:, 3, lo:hi])
+        nc.sync.dma_start(w_sb[:].bitcast(I32), w_words.rearrange("e a p n -> p (e a) n").bitcast(I32))
+        for tile, (lo, hi) in zip(gate_sb, GATE_CHUNKS):
+            nc.sync.dma_start(tile[:], gate[:, lo * C:hi * C])
+
+        staged = keep.tile([P, 7, 2 * C], BF16, name="staged")
+        slots = [keep.tile([P, C, 4], BF16, name=f"slots{e}", align_bytes=64) for e in range(E)]
+        codes = [keep.tile([P, C], U32, name=f"codes{e}", align_bytes=64) for e in range(E)]
+        scales = [keep.tile([P, C], U8, name=f"scales{e}", align_bytes=64) for e in range(E)]
+        acc = [psum.tile([P, C], F32, name=f"acc{e}") for e in range(E)]
+        y = [keep.tile([P, C], F32, name=f"y{e}") for e in range(E)]
+
+        def lst(e):
+            return offsets[:, e * C // 16:(e + 1) * C // 16]
+
+        def gather_pair(e):
+            nc.vector.tensor_copy(staged[:, LOW_AT[e], :].bitcast(U32), pairs[:].bitcast(U32).indirect(lst(e)))
+
+        def gather_row(e, row, j):
+            dst = staged[:, HIGH_AT[e], :].rearrange("p (c j) -> p c j", j=2)
+            nc.scalar.activation(dst[:, :, j], row[:].indirect(lst(e)), COPY)
+
+        def merge(e):
+            dst = slots[e][:].rearrange("p c j -> p (c j)").bitcast(F32).rearrange("p (c h) -> p c h", h=2)
+            lo, hi = LOW_AT[e], HIGH_AT[e]
+            src = staged[:].bitcast(F32)[:, lo:hi + 1:hi - lo, :].rearrange("p h c -> p c h")
+            if e == 0:
+                nc.vector.tensor_copy(dst, src)
+            else:
+                nc.scalar.copy(dst, src)
+
+        def product(e):
+            nc.vector.quantize_mx(codes[e][:].bitcast(FP8X4), scales[e][:], slots[e][:].rearrange("p c j -> p (c j)"))
+            nc.tensor.matmul_mx(acc[e][:], lhsT=w_sb[:, e, :].bitcast(FP4X4), lhsT_scale=ws_sb[:, e, :],
+                                rhs=codes[e][:].bitcast(FP8X4), rhs_scale=scales[e][:], start=True, stop=True)
+
+        def add_bias(e):
+            nc.scalar.activation(y[e][:], acc[e][:], IDENT, bias=b_sb[:, e:e + 1])
+
+        def scatter(e):
+            tile, lo = [(t, lo) for t, (lo, hi) in zip(gate_sb, GATE_CHUNKS) if lo <= e < hi][0]
+            nc.vector.tensor_tensor(result[:].indirect(lst(e)), y[e][:], tile[:, (e - lo) * C:(e - lo + 1) * C], MULT)
+
+        nc.scalar.activation(row2[:, :T], raw2[:], COPY)
+        for raw, (lo, hi) in zip(raw_pairs, PAIR_CHUNKS):
+            nc.vector.tensor_copy(
+                pairs[:, 2 * lo:2 * hi].rearrange("p (t j) -> p t j", j=2),
+                raw[:].rearrange("p j t -> p t j"),
+            )
+        for e in range(EARLY):
+            gather_row(e, row2, 0)
+        for e in range(E - 2):
+            gather_pair(e)
+        for raw, (lo, hi) in zip(raw3, LAST_ROW_CHUNKS):
+            nc.scalar.activation(row3[:, lo:hi], raw[:], COPY)
+        for e in range(EARLY):
+            gather_row(e, row3, 1)
+        merge(0)
+        product(0)
+        gather_pair(4)
+        gather_pair(5)
+        merge(1)
+        product(1)
+        add_bias(0)
+        scatter(0)
+        merge(2)
+        product(2)
+        gather_row(3, row2, 0)
+        add_bias(1)
+        scatter(1)
+        for e in range(EARLY, E):
+            gather_row(e, row3, 1)
+            if e + 1 < E:
+                gather_row(e + 1, row2, 0)
+            merge(e)
+            product(e)
+            add_bias(e - 1)
+            scatter(e - 1)
+        add_bias(E - 1)
+        scatter(E - 1)
+        nc.sync.dma_start(out, result[:, :T])

@@ -21,7 +21,7 @@ MULT = mybir.AluOpType.mult
 
 PAIR_CHUNKS = [(0, 640), (640, 1024)]
 LAST_ROW_CHUNKS = [(0, 512), (512, 1024)]
-GATE_CHUNKS = [(0, 1), (1, 3), (3, 6)]
+GATE_CHUNKS = [(0, 2), (2, 6)]
 EARLY = 3
 LOW_AT = [0, 2, 3, 4, 0, 1]
 HIGH_AT = [1, 5, 6, 5, 6, 5]
@@ -48,8 +48,11 @@ def tile_moe_pad_lin_bias_kernel(tc, xT, w_words, w_scales, b, gate, offs, out):
         result = keep.tile([P, S], F32, name="result")
 
         nc.vector.memset(pairs[:, 2 * T:].bitcast(I32), 0)
-        nc.vector.memset(ws_sb[:].rearrange("p e n -> p (e n)").bitcast(I32), 0)
-        nc.gpsimd.memset(row3[:, T:], 0.0)
+        nc.vector.memset(row3[:, T:].bitcast(I32), 0)
+        nc.gpsimd.memset(ws_sb[:].rearrange("p e n -> p (e n)").bitcast(I32), 0)
+        ws_rows = w_scales.rearrange("e a q n -> q (e a) n").bitcast(I32)
+        for quad in range(4):
+            nc.gpsimd.dma_start(ws_sb[32 * quad:32 * quad + 4].bitcast(I32), ws_rows[4 * quad:4 * quad + 4])
         nc.scalar.dma_start(b_sb[:], b)
         nc.scalar.activation(row2[:, T:], pairs[:, 2 * T:2 * T + S - T], COPY)
 
@@ -57,17 +60,14 @@ def tile_moe_pad_lin_bias_kernel(tc, xT, w_words, w_scales, b, gate, offs, out):
         nc.sync.dma_start(offsets[:], offs)
         for raw, (lo, hi) in zip(raw_pairs, PAIR_CHUNKS):
             nc.sync.dma_start(raw[:], x_rows[:, 0:2, lo:hi])
-        ws_rows = w_scales.rearrange("e a q n -> q (e a) n").bitcast(I32)
-        for quad in range(4):
-            nc.sync.dma_start(ws_sb[32 * quad:32 * quad + 4].bitcast(I32), ws_rows[4 * quad:4 * quad + 4])
         for raw, (lo, hi) in zip(raw3, LAST_ROW_CHUNKS):
             nc.sync.dma_start(raw[:], x_rows[:, 3, lo:hi])
         nc.sync.dma_start(w_sb[:].bitcast(I32), w_words.rearrange("e a p n -> p (e a) n").bitcast(I32))
         for tile, (lo, hi) in zip(gate_sb, GATE_CHUNKS):
             nc.sync.dma_start(tile[:], gate[:, lo * C:hi * C])
 
-        staged = keep.tile([P, 7, 2 * C], BF16, name="staged")
-        slots = [keep.tile([P, C, 4], BF16, name=f"slots{e}", align_bytes=64) for e in range(E)]
+        staged = keep.tile([P, 7, 2 * C], BF16, name="staged", align_bytes=64)
+        slots = [None] + [keep.tile([P, 4 * C], BF16, name=f"slots{e}", align_bytes=64) for e in range(1, E)]
         codes = [keep.tile([P, C], U32, name=f"codes{e}", align_bytes=64) for e in range(E)]
         scales = [keep.tile([P, C], U8, name=f"scales{e}", align_bytes=64) for e in range(E)]
         acc = [psum.tile([P, C], F32, name=f"acc{e}") for e in range(E)]
@@ -76,24 +76,31 @@ def tile_moe_pad_lin_bias_kernel(tc, xT, w_words, w_scales, b, gate, offs, out):
         def lst(e):
             return offsets[:, e * C // 16:(e + 1) * C // 16]
 
+        def quantiser_input(e):
+            if e == 0:
+                return staged[:, 0:2, :].rearrange("p r c -> p (r c)")
+            return slots[e][:]
+
         def gather_pair(e):
-            nc.vector.tensor_copy(staged[:, LOW_AT[e], :].bitcast(U32), pairs[:].bitcast(U32).indirect(lst(e)))
+            if e == 0:
+                dst = quantiser_input(e).bitcast(U32).rearrange("p (c h) -> p c h", h=2)[:, :, 0]
+            else:
+                dst = staged[:, LOW_AT[e], :].bitcast(U32)
+            nc.vector.tensor_copy(dst, pairs[:].bitcast(U32).indirect(lst(e)))
 
         def gather_row(e, row, j):
-            dst = staged[:, HIGH_AT[e], :].rearrange("p (c j) -> p c j", j=2)
-            nc.scalar.activation(dst[:, :, j], row[:].indirect(lst(e)), COPY)
-
-        def merge(e):
-            dst = slots[e][:].rearrange("p c j -> p (c j)").bitcast(F32).rearrange("p (c h) -> p c h", h=2)
-            lo, hi = LOW_AT[e], HIGH_AT[e]
-            src = staged[:].bitcast(F32)[:, lo:hi + 1:hi - lo, :].rearrange("p h c -> p c h")
             if e == 0:
-                nc.vector.tensor_copy(dst, src)
+                dst = quantiser_input(e).rearrange("p (c j) -> p c j", j=4)[:, :, 2 + j]
             else:
-                nc.scalar.copy(dst, src)
+                dst = staged[:, HIGH_AT[e], :].rearrange("p (c j) -> p c j", j=2)[:, :, j]
+            nc.scalar.activation(dst, row[:].indirect(lst(e)), COPY)
 
         def product(e):
-            nc.vector.quantize_mx(codes[e][:].bitcast(FP8X4), scales[e][:], slots[e][:].rearrange("p c j -> p (c j)"))
+            if e > 0:
+                lo, hi = LOW_AT[e], HIGH_AT[e]
+                src = staged[:].bitcast(F32)[:, lo:hi + 1:hi - lo, :].rearrange("p h c -> p c h")
+                nc.scalar.copy(slots[e][:].bitcast(F32).rearrange("p (c h) -> p c h", h=2), src)
+            nc.vector.quantize_mx(codes[e][:].bitcast(FP8X4), scales[e][:], quantiser_input(e))
             nc.tensor.matmul_mx(acc[e][:], lhsT=w_sb[:, e, :].bitcast(FP4X4), lhsT_scale=ws_sb[:, e, :],
                                 rhs=codes[e][:].bitcast(FP8X4), rhs_scale=scales[e][:], start=True, stop=True)
 
@@ -116,29 +123,33 @@ def tile_moe_pad_lin_bias_kernel(tc, xT, w_words, w_scales, b, gate, offs, out):
             gather_pair(e)
         for raw, (lo, hi) in zip(raw3, LAST_ROW_CHUNKS):
             nc.scalar.activation(row3[:, lo:hi], raw[:], COPY)
-        for e in range(EARLY):
-            gather_row(e, row3, 1)
-        merge(0)
+        gather_row(0, row3, 1)
+        gather_row(1, row3, 1)
         product(0)
+        gather_row(2, row3, 1)
         gather_pair(4)
         gather_pair(5)
-        merge(1)
         product(1)
         add_bias(0)
         scatter(0)
-        merge(2)
+        gather_row(3, row3, 1)
         product(2)
-        gather_row(3, row2, 0)
         add_bias(1)
         scatter(1)
-        for e in range(EARLY, E):
-            gather_row(e, row3, 1)
-            if e + 1 < E:
-                gather_row(e + 1, row2, 0)
-            merge(e)
-            product(e)
-            add_bias(e - 1)
-            scatter(e - 1)
-        add_bias(E - 1)
-        scatter(E - 1)
+        gather_row(3, row2, 0)
+        gather_row(4, row2, 0)
+        product(3)
+        add_bias(2)
+        scatter(2)
+        gather_row(4, row3, 1)
+        gather_row(5, row2, 0)
+        product(4)
+        add_bias(3)
+        scatter(3)
+        gather_row(5, row3, 1)
+        product(5)
+        add_bias(4)
+        scatter(4)
+        add_bias(5)
+        scatter(5)
         nc.sync.dma_start(out, result[:, :T])

from contextlib import ExitStack

import concourse.mybir as mybir

K, T, E, C, N = 512, 1024, 6, 256, 128
S = E * C
P = 128
FLOPS = 2 * K * N * S

F32 = mybir.dt.float32
BF16 = mybir.dt.bfloat16
I32 = mybir.dt.int32
U32 = mybir.dt.uint32
U16 = mybir.dt.uint16
U8 = mybir.dt.uint8
FP8X4 = mybir.dt.float8_e4m3fn_x4
FP4X4 = mybir.dt.float4_e2m1fn_x4
COPY = mybir.ActivationFunctionType.Copy
IDENT = mybir.ActivationFunctionType.Identity
MULT = mybir.AluOpType.mult

PAIR_CHUNKS = [(0, 640), (640, 1024)]
LAST_ROW_CHUNKS = [(0, 512), (512, 1024)]
GATE_CHUNKS = [(0, 2), (2, 6)]
EARLY = 3
LOW_AT = [0, 2, 3, 4, 0, 1]
HIGH_AT = [1, 5, 6, 5, 6, 5]


def tile_moe_pad_lin_bias_kernel(tc, xT, w_words, w_scales, b, gate, offs, out):
    nc = tc.nc
    with ExitStack() as ctx:
        keep = ctx.enter_context(tc.tile_pool(name="keep", bufs=1))
        psum = ctx.enter_context(tc.psum_pool(name="psum", bufs=1))

        x_rows = xT.rearrange("(p j) t -> p j t", j=4)
        offsets = keep.tile([P, S // 16], U16, name="offsets")
        pairs = keep.tile([P, 2 * S], BF16, name="pairs", align_bytes=64)
        row2 = keep.tile([P, S], BF16, name="row2", align_bytes=64)
        row3 = keep.tile([P, S], BF16, name="row3", align_bytes=64)
        raw_pairs = [keep.tile([P, 2, hi - lo], F32, name=f"raw_pair{lo}") for lo, hi in PAIR_CHUNKS]
        raw2 = keep.tile([P, T], F32, name="raw2")
        raw3 = [keep.tile([P, hi - lo], F32, name=f"raw3_{lo}") for lo, hi in LAST_ROW_CHUNKS]
        w_sb = keep.tile([P, E, 2 * N], U8, name="w_sb", align_bytes=64)
        ws_sb = keep.tile([P, E, N], U8, name="ws_sb", align_bytes=64)
        b_sb = keep.tile([P, E], F32, name="b_sb")
        gate_sb = [keep.tile([P, (hi - lo) * C], F32, name=f"gate{lo}") for lo, hi in GATE_CHUNKS]
        result = keep.tile([P, S], F32, name="result")

        nc.vector.memset(pairs[:, 2 * T:].bitcast(I32), 0)
        nc.vector.memset(row3[:, T:].bitcast(I32), 0)
        nc.gpsimd.memset(ws_sb[:].rearrange("p e n -> p (e n)").bitcast(I32), 0)
        ws_rows = w_scales.rearrange("e a q n -> q (e a) n").bitcast(I32)
        for quad in range(4):
            nc.gpsimd.dma_start(ws_sb[32 * quad:32 * quad + 4].bitcast(I32), ws_rows[4 * quad:4 * quad + 4])
        nc.scalar.dma_start(b_sb[:], b)
        nc.scalar.activation(row2[:, T:], pairs[:, 2 * T:2 * T + S - T], COPY)

        nc.sync.dma_start(raw2[:], x_rows[:, 2, :])
        nc.sync.dma_start(offsets[:], offs)
        for raw, (lo, hi) in zip(raw_pairs, PAIR_CHUNKS):
            nc.sync.dma_start(raw[:], x_rows[:, 0:2, lo:hi])
        for raw, (lo, hi) in zip(raw3, LAST_ROW_CHUNKS):
            nc.sync.dma_start(raw[:], x_rows[:, 3, lo:hi])
        nc.sync.dma_start(w_sb[:].bitcast(I32), w_words.rearrange("e a p n -> p (e a) n").bitcast(I32))
        for tile, (lo, hi) in zip(gate_sb, GATE_CHUNKS):
            nc.sync.dma_start(tile[:], gate[:, lo * C:hi * C])

        staged = keep.tile([P, 7, 2 * C], BF16, name="staged", align_bytes=64)
        slots = [None] + [keep.tile([P, 4 * C], BF16, name=f"slots{e}", align_bytes=64) for e in range(1, E)]
        codes = [keep.tile([P, C], U32, name=f"codes{e}", align_bytes=64) for e in range(E)]
        scales = [keep.tile([P, C], U8, name=f"scales{e}", align_bytes=64) for e in range(E)]
        acc = [psum.tile([P, C], F32, name=f"acc{e}") for e in range(E)]
        y = [keep.tile([P, C], F32, name=f"y{e}") for e in range(E)]

        def lst(e):
            return offsets[:, e * C // 16:(e + 1) * C // 16]

        def quantiser_input(e):
            if e == 0:
                return staged[:, 0:2, :].rearrange("p r c -> p (r c)")
            return slots[e][:]

        def gather_pair(e):
            if e == 0:
                dst = quantiser_input(e).bitcast(U32).rearrange("p (c h) -> p c h", h=2)[:, :, 0]
            else:
                dst = staged[:, LOW_AT[e], :].bitcast(U32)
            nc.vector.tensor_copy(dst, pairs[:].bitcast(U32).indirect(lst(e)))

        def gather_row(e, row, j):
            if e == 0:
                dst = quantiser_input(e).rearrange("p (c j) -> p c j", j=4)[:, :, 2 + j]
            else:
                dst = staged[:, HIGH_AT[e], :].rearrange("p (c j) -> p c j", j=2)[:, :, j]
            nc.scalar.activation(dst, row[:].indirect(lst(e)), COPY)

        def product(e):
            if e > 0:
                lo, hi = LOW_AT[e], HIGH_AT[e]
                src = staged[:].bitcast(F32)[:, lo:hi + 1:hi - lo, :].rearrange("p h c -> p c h")
                nc.scalar.copy(slots[e][:].bitcast(F32).rearrange("p (c h) -> p c h", h=2), src)
            nc.vector.quantize_mx(codes[e][:].bitcast(FP8X4), scales[e][:], quantiser_input(e))
            nc.tensor.matmul_mx(acc[e][:], lhsT=w_sb[:, e, :].bitcast(FP4X4), lhsT_scale=ws_sb[:, e, :],
                                rhs=codes[e][:].bitcast(FP8X4), rhs_scale=scales[e][:], start=True, stop=True)

        def add_bias(e):
            nc.scalar.activation(y[e][:], acc[e][:], IDENT, bias=b_sb[:, e:e + 1])

        def scatter(e):
            tile, lo = [(t, lo) for t, (lo, hi) in zip(gate_sb, GATE_CHUNKS) if lo <= e < hi][0]
            nc.vector.tensor_tensor(result[:].indirect(lst(e)), y[e][:], tile[:, (e - lo) * C:(e - lo + 1) * C], MULT)

        nc.scalar.activation(row2[:, :T], raw2[:], COPY)
        for raw, (lo, hi) in zip(raw_pairs, PAIR_CHUNKS):
            nc.vector.tensor_copy(
                pairs[:, 2 * lo:2 * hi].rearrange("p (t j) -> p t j", j=2),
                raw[:].rearrange("p j t -> p t j"),
            )
        for e in range(EARLY):
            gather_row(e, row2, 0)
        for e in range(E - 2):
            gather_pair(e)
        for raw, (lo, hi) in zip(raw3, LAST_ROW_CHUNKS):
            nc.scalar.activation(row3[:, lo:hi], raw[:], COPY)
        gather_row(0, row3, 1)
        gather_row(1, row3, 1)
        product(0)
        gather_row(2, row3, 1)
        gather_pair(4)
        gather_pair(5)
        product(1)
        add_bias(0)
        scatter(0)
        gather_row(3, row3, 1)
        product(2)
        add_bias(1)
        scatter(1)
        gather_row(3, row2, 0)
        gather_row(4, row2, 0)
        product(3)
        add_bias(2)
        scatter(2)
        gather_row(4, row3, 1)
        gather_row(5, row2, 0)
        product(4)
        add_bias(3)
        scatter(3)
        gather_row(5, row3, 1)
        product(5)
        add_bias(4)
        scatter(4)
        add_bias(5)
        scatter(5)
        nc.sync.dma_start(out, result[:, :T])
